import numpy as np
import ml_dtypes


def mxq(x, axis, fmt="e4m3"):
    dtype, down = {"e4m3": (ml_dtypes.float8_e4m3fn, 7), "e5m2": (ml_dtypes.float8_e5m2, 14)}[fmt]
    v = np.moveaxis(np.asarray(x, np.float32).astype(ml_dtypes.bfloat16).astype(np.float64), axis, -1)
    blocks = v.reshape(v.shape[:-1] + (-1, 32))
    amax = np.abs(blocks).max(-1, keepdims=True)
    byte = np.maximum(np.where(amax > 0, np.frexp(amax)[1] - 1 + 127, 0) - down, 1)
    scale = np.exp2(byte - 127.0)
    codes = (blocks / scale).astype(np.float32).astype(dtype).astype(np.float64)
    return np.moveaxis((codes * scale).reshape(v.shape), -1, axis)


WIDE = False


def mx_kscale(k):
    if not WIDE:
        return np.ones(k)
    levels = np.array([30, -30])
    if k % 512:
        return np.exp2(np.random.permutation(np.resize(levels, k // 32))).repeat(32)
    a = np.empty((k // 512, 16))
    for p in range(k // 512):
        a[p, :8] = np.random.permutation(np.resize(levels, 8))
        for g in range(8):
            far = levels[np.abs(levels - a[p, g]) >= 10]
            a[p, g + 8] = far[np.random.randint(len(far))]
    return np.exp2(a.ravel()).repeat(32)


def f64(x):
    return np.asarray(x).astype(np.float64)


def striped(idx):
    return np.tile(np.asarray(idx).reshape(-1, 16).T, (8, 1)).astype(np.uint16)


def unstriped(offs):
    return offs[:16].T.reshape(-1).astype(np.int64)


E2M1 = np.array([0.0, 0.5, 1.0, 1.5, 2.0, 3.0, 4.0, 6.0, -0.0, -0.5, -1.0, -1.5, -2.0, -3.0, -4.0, -6.0])


def pack_weight(w, fmt):
    k, n = w.shape
    w = f64(np.asarray(w, np.float32).astype(ml_dtypes.bfloat16)).reshape(k // 32, 32, n)
    amax = np.abs(w).max(1)
    if fmt in ("e4m3", "e5m2"):
        byte = np.frexp(amax)[1] - 1 + 127 - (7 if fmt == "e4m3" else 14)
    else:
        mant, ex = np.frexp(amax / 6.0)
        byte = np.where(mant > 0.5, ex, ex - 1) + 127
    byte = np.clip(np.where(amax > 0, byte, 1), 1, 254)
    scaled = (w * np.exp2(127.0 - byte)[:, None, :]).reshape(k, n).astype(np.float32)
    by_word = np.ascontiguousarray(scaled.reshape(k // 512, 128, 4, n).transpose(0, 1, 3, 2))
    if fmt in ("e4m3", "e5m2"):
        words = by_word.astype(ml_dtypes.float8_e4m3fn if fmt == "e4m3" else ml_dtypes.float8_e5m2).view(np.uint8)
    else:
        c = by_word.astype(ml_dtypes.float4_e2m1fn).view(np.uint8) & 0xF
        words = (c[..., 0::2] | (c[..., 1::2] << 4)).reshape(k // 512, 128, 2 * n)
    return np.ascontiguousarray(words), np.ascontiguousarray(byte.astype(np.uint8).reshape(k // 512, 16, n))


def unpack_weight(words, scales, fmt):
    g, _, n = scales.shape
    words = np.ascontiguousarray(words).reshape(g, 128, n, -1)
    if fmt in ("e4m3", "e5m2"):
        vals = words.view(ml_dtypes.float8_e4m3fn if fmt == "e4m3" else ml_dtypes.float8_e5m2).astype(np.float64)
    else:
        nib = np.empty((g, 128, n, 4), np.uint8)
        nib[..., 0::2] = words & 0xF
        nib[..., 1::2] = words >> 4
        vals = E2M1[nib]
    vals = vals * np.repeat(np.exp2(scales.astype(np.float64) - 127.0), 8, axis=1)[..., None]
    return vals.transpose(0, 1, 3, 2).reshape(g * 512, n)


K, J, N, R, T, V, Q = 512, 512, 256, 256, 1024, 1024, 1024


def setup_inputs():
    n = np.random.standard_normal
    idx = np.random.permutation(T)[:J]
    idx2 = np.random.permutation(V)[:J]
    idx3 = np.random.permutation(V)[:J]
    idx4 = np.random.permutation(Q)[:N]
    fj = mx_kscale(J)
    fk = mx_kscale(K)
    drp = pack_weight(n((K, R)) * 1 / np.sqrt(K) / fk[:, None], "e5m2")
    return {
        "xf": (n((K, T))).astype(np.float32),
        "ra": (np.random.uniform(0.5, 1.5, (1, J)) * fj).astype(np.float32),
        "ow": (n((K, J)) * 0.7).astype(np.float32),
        "gt": (n((N, V)) * np.exp(0.5 * n((1, V)))).astype(np.float32),
        "rb": (np.random.uniform(0.5, 1.5, (1, J)) / fj).astype(np.float32),
        "fkr": (np.random.uniform(0.5, 1.5, (1, K)) * fk).astype(np.float32),
        "dr_words": drp[0],
        "dr_scales": drp[1],
        "old": (0.5 * n((R, Q))).astype(np.float32),
        "offs": striped(idx),
        "offs2": striped(idx2),
        "offs3": striped(idx3),
        "offs4": striped(idx4),
    }


def reference(xf, ra, ow, gt, rb, fkr, dr_words, dr_scales, old, offs, offs2, offs3, offs4):
    idx = unstriped(offs)
    idx2 = unstriped(offs2)
    idx3 = unstriped(offs3)
    idx4 = unstriped(offs4)
    dru = unpack_weight(dr_words, dr_scales, "e5m2")
    us = (f64(xf)[:, idx] - f64(ow)) * f64(ra)
    ut = us.T
    uj = ut * f64(fkr)
    gs = (f64(gt)[:, idx2] - 0.7 * f64(gt)[:, idx3]) * f64(rb)
    gj = gs.T
    ujq = mxq(uj, 0, "e4m3")
    gjq = mxq(gj, 0, "e5m2")
    w = ujq.T @ gjq
    wq = mxq(w, 0, "e5m2")
    v2 = dru.T @ wq
    wp = np.zeros((R, Q))
    wp[:, idx4] = v2
    y = 0.05 * wp + f64(old)
    return y

@@ -1,0 +1,258 @@
+from contextlib import ExitStack
+
+import concourse.mybir as mybir
+from concourse.masks import make_identity
+
+K, J, N, R, T, V, Q = 512, 512, 256, 256, 1024, 1024, 1024
+FLOPS = 2 * J * K * N + 2 * K * R * N
+
+F32 = mybir.dt.float32
+BF16 = mybir.dt.bfloat16
+I32 = mybir.dt.int32
+U32 = mybir.dt.uint32
+U16 = mybir.dt.uint16
+U8 = mybir.dt.uint8
+E4M3 = mybir.dt.float8_e4m3fn_x4
+E5M2 = mybir.dt.float8_e5m2_x4
+MULT = mybir.AluOpType.mult
+ADD = mybir.AluOpType.add
+SUB = mybir.AluOpType.subtract
+COPY = mybir.ActivationFunctionType.Copy
+
+P = 128
+PACK = 4
+LIST_ROWS = 16
+STORE_COLS = 512
+SLOT = 4096
+HALF = SLOT // 2
+PLACES = {
+    "ident_bf": 0, "g3_0": 0,
+    "diff3": HALF, "g2_1": HALF,
+    "gt0": SLOT, "picked0": SLOT,
+    "xf0": 2 * SLOT, "picked1": 2 * SLOT,
+    "xf1": 3 * SLOT, "picked2": 3 * SLOT, "uj0": 3 * SLOT + HALF,
+    "xf2": 4 * SLOT, "picked3": 4 * SLOT, "uj1": 4 * SLOT + HALF,
+    "xf3": 5 * SLOT, "g3_1": 5 * SLOT, "uj2": 5 * SLOT + HALF,
+}
+
+
+def tile_list_directions_offset_differences_placed_kernel(
+    tc, xf, ra, ow, gt, rb, fkr, dr_words, dr_scales, old, offs, offs2, offs3, offs4, out
+):
+    nc = tc.nc
+    n_tiles = N // P
+    r_tiles = R // P
+
+    with ExitStack() as ctx:
+        keep = ctx.enter_context(tc.tile_pool(name="keep", bufs=1))
+        psum = ctx.enter_context(tc.psum_pool(name="psum", bufs=1))
+
+        reuse = ctx.enter_context(tc.tile_pool(name="reuse", bufs=1))
+
+        def sb(name, shape, dtype):
+            if name in PLACES:
+                return reuse.tile(shape, dtype, name=name, align_bytes=64, offset=PLACES[name])
+            return keep.tile(shape, dtype, name=name, align_bytes=64)
+
+        idx = sb("idx", [P, J // LIST_ROWS], U16)
+        idx2 = sb("idx2", [P, J // LIST_ROWS], U16)
+        idx3 = sb("idx3", [P, J // LIST_ROWS], U16)
+        idx4 = sb("idx4", [P, N // LIST_ROWS], U16)
+        gt_sb = [sb(f"gt{h}", [P, V], F32) for h in range(n_tiles)]
+        xf_sb = [sb(f"xf{t}", [P, T], F32) for t in range(PACK)]
+        ow_sb = [sb(f"ow{t}", [P, J], F32) for t in range(PACK)]
+        old_sb = [sb(f"old{r}", [P, Q], F32) for r in range(r_tiles)]
+        ra_sb = sb("ra_sb", [P, PACK], F32)
+        rb_sb = sb("rb_sb", [P, PACK], F32)
+        fk_sb = sb("fk_sb", [P, PACK], F32)
+        dr_codes = sb("dr_codes", [P, R], U32)
+        dr_plane = sb("dr_plane", [P, R], U8)
+        ident = sb("ident", [P, P], F32)
+        pages = [sb(f"page{r}", [P, Q], F32) for r in range(r_tiles)]
+
+        ident_bf = sb("ident_bf", [P, P], BF16)
+        make_identity(nc, ident_bf[:])
+        nc.scalar.activation(ident[:], ident_bf[:], COPY)
+        nc.gpsimd.memset(dr_plane[:].bitcast(I32), 0)
+        for r in range(r_tiles):
+            nc.vector.memset(pages[r][:], 0.0)
+
+        xf_rows = xf.rearrange("(p t) c -> t p c", t=PACK)
+        ow_rows = ow.rearrange("(p t) c -> t p c", t=PACK)
+        nc.sync.dma_start(out=idx3[:], in_=offs3)
+        nc.sync.dma_start(out=idx2[:], in_=offs2)
+        nc.sync.dma_start(out=gt_sb[0][:], in_=gt[0:P, :])
+        nc.sync.dma_start(out=idx[:], in_=offs)
+        nc.sync.dma_start(out=xf_sb[0][:], in_=xf_rows[0])
+        nc.sync.dma_start(out=ra_sb[:], in_=ra.rearrange("o (p t) -> (o p) t", t=PACK))
+        nc.sync.dma_start(out=ow_sb[0][:], in_=ow_rows[0])
+        nc.sync.dma_start(out=rb_sb[:], in_=rb.rearrange("o (p t) -> (o p) t", t=PACK))
+        nc.sync.dma_start(out=fk_sb[:], in_=fkr.rearrange("o (p t) -> (o p) t", t=PACK))
+        for t in range(1, PACK):
+            nc.sync.dma_start(out=xf_sb[t][:], in_=xf_rows[t])
+            nc.sync.dma_start(out=ow_sb[t][:], in_=ow_rows[t])
+        nc.sync.dma_start(out=gt_sb[1][:], in_=gt[P:N, :])
+        nc.sync.dma_start(out=idx4[:], in_=offs4)
+        nc.sync.dma_start(
+            out=dr_codes[:].bitcast(I32), in_=dr_words[0].rearrange("p c b -> p (c b)").bitcast(I32)
+        )
+        for quad in range(4):
+            nc.sync.dma_start(
+                out=dr_plane[32 * quad : 32 * quad + 4, :].bitcast(I32),
+                in_=dr_scales[0, 4 * quad : 4 * quad + 4, :].bitcast(I32),
+            )
+        for r in range(r_tiles):
+            nc.sync.dma_start(out=old_sb[r][:], in_=old[r * P : (r + 1) * P, :])
+
+        ra_all = psum.tile([P, PACK, P], F32, name="ra_all", tag="ra_all")
+        for t in range(PACK):
+            nc.tensor.transpose(ra_all[:, t, :], ra_sb[:, t : t + 1].to_broadcast([P, P]), ident[:])
+
+        g_codes = [sb(f"g_codes{h}", [P, P], U32) for h in range(n_tiles)]
+        g_plane = [sb(f"g_plane{h}", [P, P], U8) for h in range(n_tiles)]
+        u_codes = [sb(f"u_codes{t}", [P, P], U32) for t in range(PACK)]
+        u_plane = [sb(f"u_plane{t}", [P, P], U8) for t in range(PACK)]
+        w_acc = [psum.tile([P, PACK, P], F32, name=f"w_acc{h}") for h in range(n_tiles)]
+
+        def pick_gradients(h):
+            g3 = sb(f"g3_{h}", [P, J], F32)
+            nc.scalar.activation(g3[:], gt_sb[h][:].indirect(idx3[:]), COPY, scale=-0.7)
+            g2 = sb(f"g2_{h}", [P, J], F32)
+            nc.vector.tensor_copy(g2[:], gt_sb[h][:].indirect(idx2[:]))
+            return g2, g3
+
+        def turn_adding(g2, g3):
+            bank = psum.tile([P, PACK, P], F32, name="g_turned0", tag="g_turned")
+            for t in range(PACK):
+                nc.tensor.matmul(bank[:, t, :], g2[:, t::PACK], ident[:], start=True, stop=False, is_transpose=True)
+                nc.tensor.matmul(bank[:, t, :], g3[:, t::PACK], ident[:], start=False, stop=True, is_transpose=True)
+            return bank
+
+        def add_then_turn(g2, g3):
+            total = sb("g_total", [P, PACK, P], F32)
+            nc.vector.tensor_tensor(
+                total[:].rearrange("p t q -> p q t"),
+                g2[:].rearrange("p (q t) -> p q t", t=PACK),
+                g3[:].rearrange("p (q t) -> p q t", t=PACK),
+                ADD,
+            )
+            bank = psum.tile([P, PACK, P], F32, name="g_turned1", tag="g_turned")
+            for t in range(PACK):
+                nc.tensor.transpose(bank[:, t, :], total[:, t, :], ident[:])
+            return bank
+
+        def quantise_gradients(h, bank):
+            gj = sb(f"gj{h}", [P, P, PACK], BF16)
+            nc.vector.tensor_tensor(
+                gj[:], bank[:].rearrange("p t n -> p n t"), rb_sb[:].unsqueeze(1).to_broadcast([P, P, PACK]), MULT
+            )
+            nc.vector.quantize_mx(
+                out=g_codes[h][:].bitcast(E5M2), scales=g_plane[h][:], in_=gj[:].rearrange("p n t -> p (n t)")
+            )
+
+        def weigh_features(t):
+            picked = sb(f"picked{t}", [P, J], F32)
+            diff = sb(f"diff{t}", [P, J], F32)
+            us = sb(f"us{t}", [P, J], BF16)
+            parts = 2 if t == PACK - 1 else 1
+            width = J // parts
+            for part in range(parts):
+                cols = slice(part * width, (part + 1) * width)
+                lcols = slice(part * width // LIST_ROWS, (part + 1) * width // LIST_ROWS)
+                pcols = slice(part * width // PACK, (part + 1) * width // PACK)
+                nc.scalar.activation(picked[:, cols], xf_sb[t][:].indirect(idx[:, lcols]), COPY)
+                nc.vector.tensor_tensor(diff[:, cols], picked[:, cols], ow_sb[t][:, cols], SUB)
+                nc.vector.scalar_tensor_tensor(
+                    us[:, cols].rearrange("p (q i) -> p q i", i=PACK),
+                    diff[:, cols].rearrange("p (q i) -> p q i", i=PACK),
+                    fk_sb[:, t : t + 1],
+                    ra_all[:, :, pcols].rearrange("p i q -> p q i"),
+                    MULT,
+                    MULT,
+                )
+            bank = psum.tile([P, 2, P], F32, name=f"u_turned{t}", tag=f"u_turned{t % 3}")
+            words = us[:].bitcast(F32)
+            for u in range(2):
+                nc.tensor.transpose(bank[:, u, :], words[:, u::2], ident[:])
+            return bank
+
+        def quantise_features(t, bank):
+            uj = sb(f"uj{t}", [P, P * PACK], BF16)
+            nc.scalar.copy(uj[:].bitcast(F32).rearrange("p (k u) -> p k u", u=2), bank[:].rearrange("p u k -> p k u"))
+            nc.vector.quantize_mx(out=u_codes[t][:].bitcast(E4M3), scales=u_plane[t][:], in_=uj[:])
+
+        def first_product(t, h):
+            nc.tensor.matmul_mx(
+                out=w_acc[h][:, t, :],
+                lhsT=u_codes[t][:].bitcast(E4M3),
+                lhsT_scale=u_plane[t][:],
+                rhs=g_codes[h][:].bitcast(E5M2),
+                rhs_scale=g_plane[h][:],
+                start=True,
+                stop=True,
+            )
+
+        def quantise_moment(h, copy):
+            w_bf = sb(f"w_bf{h}", [P, P, PACK], BF16)
+            copy(w_bf[:], w_acc[h][:].rearrange("p t n -> p n t"))
+            codes = sb(f"w_codes{h}", [P, P], U32)
+            plane = sb(f"w_plane{h}", [P, P], U8)
+            nc.vector.quantize_mx(out=codes[:].bitcast(E5M2), scales=plane[:], in_=w_bf[:].rearrange("p n t -> p (n t)"))
+            return codes, plane
+
+        def second_product(acc, r, codes, plane):
+            rows = slice(r * P, (r + 1) * P)
+            nc.tensor.matmul_mx(
+                out=acc,
+                lhsT=dr_codes[:, rows].bitcast(E5M2),
+                lhsT_scale=dr_plane[:, rows],
+                rhs=codes[:].bitcast(E5M2),
+                rhs_scale=plane[:],
+                start=True,
+                stop=True,
+            )
+
+        list_cols = P // LIST_ROWS
+
+        g_bank = turn_adding(*pick_gradients(0))
+        u_bank = weigh_features(0)
+        quantise_gradients(0, g_bank)
+        for t in range(PACK):
+            next_bank = weigh_features(t + 1) if t + 1 < PACK else None
+            if next_bank is None:
+                last_picks = pick_gradients(1)
+            quantise_features(t, u_bank)
+            first_product(t, 0)
+            u_bank = next_bank
+
+        g_bank = add_then_turn(*last_picks)
+
+        codes, plane = quantise_moment(0, nc.scalar.copy)
+        acc = psum.tile([P, r_tiles, P], F32, name="v2_first", tag="u_turned1")
+        for r in range(r_tiles):
+            second_product(acc[:, r, :], r, codes, plane)
+        v2_first = sb("v2_first_sb", [P, r_tiles, P], F32)
+        nc.scalar.copy(v2_first[:], acc[:])
+
+        quantise_gradients(1, g_bank)
+        for t in range(PACK):
+            first_product(t, 1)
+        for r in range(r_tiles):
+            nc.scalar.activation(pages[r][:].indirect(idx4[:, 0:list_cols]), v2_first[:, r, :], COPY)
+
+        codes, plane = quantise_moment(1, nc.vector.tensor_copy)
+        accs = [psum.tile([P, P], F32, name=f"v2_last{r}", tag=("ra_all", "u_turned2")[r]) for r in range(r_tiles)]
+        v2_last = [sb(f"v2_last_sb{r}", [P, P], F32) for r in range(r_tiles)]
+        for r in range(r_tiles):
+            second_product(accs[r][:], r, codes, plane)
+        nc.vector.tensor_copy(v2_last[0][:], accs[0][:])
+        nc.scalar.copy(v2_last[1][:], accs[1][:])
+        nc.vector.tensor_copy(pages[0][:].indirect(idx4[:, list_cols : 2 * list_cols]), v2_last[0][:])
+        nc.scalar.activation(pages[1][:].indirect(idx4[:, list_cols : 2 * list_cols]), v2_last[1][:], COPY)
+
+        for r in range(r_tiles):
+            for c0 in range(0, Q, STORE_COLS):
+                cols = slice(c0, c0 + STORE_COLS)
+                res = sb(f"res{r}_{c0}", [P, STORE_COLS], F32)
+                nc.vector.scalar_tensor_tensor(res[:], pages[r][:, cols], 0.05, old_sb[r][:, cols], MULT, ADD)
+                nc.sync.dma_start(out=out[r * P : (r + 1) * P, cols], in_=res[:])

@@ -1,7 +1,6 @@
 from contextlib import ExitStack
 
 import concourse.mybir as mybir
-from concourse.masks import make_identity
 
 K, J, N, R, T, V, Q = 512, 512, 256, 256, 1024, 1024, 1024
 FLOPS = 2 * J * K * N + 2 * K * R * N
@@ -22,17 +21,24 @@ COPY = mybir.ActivationFunctionType.Copy
 P = 128
 PACK = 4
 LIST_ROWS = 16
-STORE_COLS = 512
+STORE_CUTS = (((0, 512), (512, 1024)), ((0, 512), (512, 896), (896, 1024)))
+QUAD = 32
 SLOT = 4096
 HALF = SLOT // 2
+KB = 1024
 PLACES = {
-    "ident_bf": 0, "g3_0": 0,
-    "diff3": HALF, "g2_1": HALF,
-    "gt0": SLOT, "picked0": SLOT,
-    "xf0": 2 * SLOT, "picked1": 2 * SLOT,
-    "xf1": 3 * SLOT, "picked2": 3 * SLOT, "uj0": 3 * SLOT + HALF,
-    "xf2": 4 * SLOT, "picked3": 4 * SLOT, "uj1": 4 * SLOT + HALF,
-    "xf3": 5 * SLOT, "g3_1": 5 * SLOT, "uj2": 5 * SLOT + HALF,
+    "block": 0, "g3_0": 0,
+    "col": 28 * KB, "page0": 28 * KB,
+    "row": 32 * KB, "page1": 32 * KB,
+    "g3_1": 26 * KB, "u_codes2": 26 * KB, "u_codes3": 27 * KB,
+    "diff0": 2 * KB, "gj0": 2 * KB,
+    "ow1": 4 * KB, "g_codes0": 4 * KB,
+    "ow2": 6 * KB, "u_codes0": 6 * KB,
+    "ow3": 8 * KB, "u_codes1": 8 * KB,
+    "diff3": 10 * KB, "g2_1": 10 * KB,
+    "xf2": 12 * KB, "uj0": 12 * KB,
+    "xf3": 16 * KB, "uj1": 16 * KB,
+    "gt1": 20 * KB, "uj2": 20 * KB, "uj3": 21 * KB,
 }
 
 
@@ -70,21 +76,30 @@ def tile_list_directions_offset_differences_placed_kernel(
         ident = sb("ident", [P, P], F32)
         pages = [sb(f"page{r}", [P, Q], F32) for r in range(r_tiles)]
 
-        ident_bf = sb("ident_bf", [P, P], BF16)
-        make_identity(nc, ident_bf[:])
-        nc.scalar.activation(ident[:], ident_bf[:], COPY)
+        ones = sb("ones", [P, QUAD], F32)
+        col = sb("col", [P, QUAD], F32)
+        row = sb("row", [P, QUAD], F32)
+        block = sb("block", [P, QUAD], F32)
+        nc.vector.memset(ones[:], 1.0)
+        nc.vector.memset(ident[:], 0.0)
+        nc.vector.tensor_tensor_scan(col[:], ones[:], ones[:], 0.0, MULT, ADD)
+        nc.vector.transpose(row[:], col[:])
+        nc.vector.tensor_tensor(block[:], col[:], row[:], mybir.AluOpType.is_equal)
+        for quad in range(P // QUAD):
+            part = slice(quad * QUAD, (quad + 1) * QUAD)
+            nc.scalar.activation(ident[part, part], block[part, :], COPY)
         nc.gpsimd.memset(dr_plane[:].bitcast(I32), 0)
         for r in range(r_tiles):
             nc.vector.memset(pages[r][:], 0.0)
 
         xf_rows = xf.rearrange("(p t) c -> t p c", t=PACK)
         ow_rows = ow.rearrange("(p t) c -> t p c", t=PACK)
+        nc.sync.dma_start(out=ra_sb[:], in_=ra.rearrange("o (p t) -> (o p) t", t=PACK))
         nc.sync.dma_start(out=idx3[:], in_=offs3)
         nc.sync.dma_start(out=idx2[:], in_=offs2)
         nc.sync.dma_start(out=gt_sb[0][:], in_=gt[0:P, :])
         nc.sync.dma_start(out=idx[:], in_=offs)
         nc.sync.dma_start(out=xf_sb[0][:], in_=xf_rows[0])
-        nc.sync.dma_start(out=ra_sb[:], in_=ra.rearrange("o (p t) -> (o p) t", t=PACK))
         nc.sync.dma_start(out=ow_sb[0][:], in_=ow_rows[0])
         nc.sync.dma_start(out=rb_sb[:], in_=rb.rearrange("o (p t) -> (o p) t", t=PACK))
         nc.sync.dma_start(out=fk_sb[:], in_=fkr.rearrange("o (p t) -> (o p) t", t=PACK))
@@ -114,12 +129,23 @@ def tile_list_directions_offset_differences_placed_kernel(
         u_plane = [sb(f"u_plane{t}", [P, P], U8) for t in range(PACK)]
         w_acc = [psum.tile([P, PACK, P], F32, name=f"w_acc{h}") for h in range(n_tiles)]
 
-        def pick_gradients(h):
+        def pick_subtrahend(h):
             g3 = sb(f"g3_{h}", [P, J], F32)
             nc.scalar.activation(g3[:], gt_sb[h][:].indirect(idx3[:]), COPY, scale=-0.7)
+            return g3
+
+        def pick_minuend(h):
             g2 = sb(f"g2_{h}", [P, J], F32)
             nc.vector.tensor_copy(g2[:], gt_sb[h][:].indirect(idx2[:]))
-            return g2, g3
+            return g2
+
+        def pick_minuend_shared(h):
+            half = J // 2
+            lhalf = half // LIST_ROWS
+            g2 = sb(f"g2_{h}", [P, J], F32)
+            nc.vector.tensor_copy(g2[:, 0:half], gt_sb[h][:].indirect(idx2[:, 0:lhalf]))
+            nc.scalar.activation(g2[:, half:J], gt_sb[h][:].indirect(idx2[:, lhalf : 2 * lhalf]), COPY)
+            return g2
 
         def turn_adding(g2, g3):
             bank = psum.tile([P, PACK, P], F32, name="g_turned0", tag="g_turned")
@@ -141,35 +167,41 @@ def tile_list_directions_offset_differences_placed_kernel(
                 nc.tensor.transpose(bank[:, t, :], total[:, t, :], ident[:])
             return bank
 
-        def quantise_gradients(h, bank):
+        def weigh_gradients(h, bank):
             gj = sb(f"gj{h}", [P, P, PACK], BF16)
             nc.vector.tensor_tensor(
                 gj[:], bank[:].rearrange("p t n -> p n t"), rb_sb[:].unsqueeze(1).to_broadcast([P, P, PACK]), MULT
             )
+            return gj
+
+        def quantise_gradients(h, gj):
             nc.vector.quantize_mx(
                 out=g_codes[h][:].bitcast(E5M2), scales=g_plane[h][:], in_=gj[:].rearrange("p n t -> p (n t)")
             )
 
-        def weigh_features(t):
+        def subtract_features(t):
             picked = sb(f"picked{t}", [P, J], F32)
             diff = sb(f"diff{t}", [P, J], F32)
+            if t == 0:
+                half = J // 2
+                lhalf = half // LIST_ROWS
+                nc.vector.tensor_copy(picked[:, 0:half], xf_sb[t][:].indirect(idx[:, 0:lhalf]))
+                nc.scalar.activation(picked[:, half:J], xf_sb[t][:].indirect(idx[:, lhalf : 2 * lhalf]), COPY)
+            else:
+                nc.scalar.activation(picked[:], xf_sb[t][:].indirect(idx[:]), COPY)
+            nc.vector.tensor_tensor(diff[:], picked[:], ow_sb[t][:], SUB)
+            return diff
+
+        def weigh_features(t, diff):
             us = sb(f"us{t}", [P, J], BF16)
-            parts = 2 if t == PACK - 1 else 1
-            width = J // parts
-            for part in range(parts):
-                cols = slice(part * width, (part + 1) * width)
-                lcols = slice(part * width // LIST_ROWS, (part + 1) * width // LIST_ROWS)
-                pcols = slice(part * width // PACK, (part + 1) * width // PACK)
-                nc.scalar.activation(picked[:, cols], xf_sb[t][:].indirect(idx[:, lcols]), COPY)
-                nc.vector.tensor_tensor(diff[:, cols], picked[:, cols], ow_sb[t][:, cols], SUB)
-                nc.vector.scalar_tensor_tensor(
-                    us[:, cols].rearrange("p (q i) -> p q i", i=PACK),
-                    diff[:, cols].rearrange("p (q i) -> p q i", i=PACK),
-                    fk_sb[:, t : t + 1],
-                    ra_all[:, :, pcols].rearrange("p i q -> p q i"),
-                    MULT,
-                    MULT,
-                )
+            nc.vector.scalar_tensor_tensor(
+                us[:].rearrange("p (q i) -> p q i", i=PACK),
+                diff[:].rearrange("p (q i) -> p q i", i=PACK),
+                fk_sb[:, t : t + 1],
+                ra_all[:].rearrange("p i q -> p q i"),
+                MULT,
+                MULT,
+            )
             bank = psum.tile([P, 2, P], F32, name=f"u_turned{t}", tag=f"u_turned{t % 3}")
             words = us[:].bitcast(F32)
             for u in range(2):
@@ -214,18 +246,22 @@ def tile_list_directions_offset_differences_placed_kernel(
 
         list_cols = P // LIST_ROWS
 
-        g_bank = turn_adding(*pick_gradients(0))
-        u_bank = weigh_features(0)
-        quantise_gradients(0, g_bank)
-        for t in range(PACK):
-            next_bank = weigh_features(t + 1) if t + 1 < PACK else None
-            if next_bank is None:
-                last_picks = pick_gradients(1)
-            quantise_features(t, u_bank)
+        g_bank = turn_adding(pick_minuend(0), pick_subtrahend(0))
+        u_banks = [weigh_features(0, subtract_features(0))]
+        gj = weigh_gradients(0, g_bank)
+        diff = subtract_features(1)
+        quantise_gradients(0, gj)
+        u_banks.append(weigh_features(1, diff))
+        for t in range(2):
+            diff = subtract_features(t + 2)
+            quantise_features(t, u_banks[t])
+            u_banks.append(weigh_features(t + 2, diff))
             first_product(t, 0)
-            u_bank = next_bank
-
-        g_bank = add_then_turn(*last_picks)
+        subtrahend = pick_subtrahend(1)
+        last_bank = add_then_turn(pick_minuend_shared(1), subtrahend)
+        for t in range(2, PACK):
+            quantise_features(t, u_banks[t])
+            first_product(t, 0)
 
         codes, plane = quantise_moment(0, nc.scalar.copy)
         acc = psum.tile([P, r_tiles, P], F32, name="v2_first", tag="u_turned1")
@@ -234,7 +270,7 @@ def tile_list_directions_offset_differences_placed_kernel(
         v2_first = sb("v2_first_sb", [P, r_tiles, P], F32)
         nc.scalar.copy(v2_first[:], acc[:])
 
-        quantise_gradients(1, g_bank)
+        quantise_gradients(1, weigh_gradients(1, last_bank))
         for t in range(PACK):
             first_product(t, 1)
         for r in range(r_tiles):
@@ -251,8 +287,8 @@ def tile_list_directions_offset_differences_placed_kernel(
         nc.scalar.activation(pages[1][:].indirect(idx4[:, list_cols : 2 * list_cols]), v2_last[1][:], COPY)
 
         for r in range(r_tiles):
-            for c0 in range(0, Q, STORE_COLS):
-                cols = slice(c0, c0 + STORE_COLS)
-                res = sb(f"res{r}_{c0}", [P, STORE_COLS], F32)
+            for c0, c1 in STORE_CUTS[r]:
+                cols = slice(c0, c1)
+                res = sb(f"res{r}_{c0}", [P, c1 - c0], F32)
                 nc.vector.scalar_tensor_tensor(res[:], pages[r][:, cols], 0.05, old_sb[r][:, cols], MULT, ADD)
                 nc.sync.dma_start(out=out[r * P : (r + 1) * P, cols], in_=res[:])

@@ -28,17 +28,13 @@ HALF = SLOT // 2
 KB = 1024
 PLACES = {
     "block": 0, "g3_0": 0,
+    "diff0": 2 * KB, "gj0": 2 * KB,
+    "diff2": 4 * KB, "u_codes0": 4 * KB,
+    "diff3": 6 * KB, "gj1": 6 * KB, "u_codes1": 7 * KB, "u_codes2": 7 * KB + 512,
+    "xf2": 12 * KB, "uj0": 12 * KB,
+    "xf3": 16 * KB, "uj1": 16 * KB, "uj2": 17 * KB,
     "col": 28 * KB, "page0": 28 * KB,
     "row": 32 * KB, "page1": 32 * KB,
-    "g3_1": 26 * KB, "u_codes2": 26 * KB, "u_codes3": 27 * KB,
-    "diff0": 2 * KB, "gj0": 2 * KB,
-    "ow1": 4 * KB, "g_codes0": 4 * KB,
-    "ow2": 6 * KB, "u_codes0": 6 * KB,
-    "ow3": 8 * KB, "u_codes1": 8 * KB,
-    "diff3": 10 * KB, "g2_1": 10 * KB,
-    "xf2": 12 * KB, "uj0": 12 * KB,
-    "xf3": 16 * KB, "uj1": 16 * KB,
-    "gt1": 20 * KB, "uj2": 20 * KB, "uj3": 21 * KB,
 }
 
 
@@ -97,7 +93,8 @@ def tile_list_directions_offset_differences_placed_kernel(
         nc.sync.dma_start(out=ra_sb[:], in_=ra.rearrange("o (p t) -> (o p) t", t=PACK))
         nc.sync.dma_start(out=idx3[:], in_=offs3)
         nc.sync.dma_start(out=idx2[:], in_=offs2)
-        nc.sync.dma_start(out=gt_sb[0][:], in_=gt[0:P, :])
+        for h in range(n_tiles):
+            nc.sync.dma_start(out=gt_sb[h][:], in_=gt[h * P : (h + 1) * P, :])
         nc.sync.dma_start(out=idx[:], in_=offs)
         nc.sync.dma_start(out=xf_sb[0][:], in_=xf_rows[0])
         nc.sync.dma_start(out=ow_sb[0][:], in_=ow_rows[0])
@@ -106,7 +103,6 @@ def tile_list_directions_offset_differences_placed_kernel(
         for t in range(1, PACK):
             nc.sync.dma_start(out=xf_sb[t][:], in_=xf_rows[t])
             nc.sync.dma_start(out=ow_sb[t][:], in_=ow_rows[t])
-        nc.sync.dma_start(out=gt_sb[1][:], in_=gt[P:N, :])
         nc.sync.dma_start(out=idx4[:], in_=offs4)
         nc.sync.dma_start(
             out=dr_codes[:].bitcast(I32), in_=dr_words[0].rearrange("p c b -> p (c b)").bitcast(I32)
@@ -139,32 +135,11 @@ def tile_list_directions_offset_differences_placed_kernel(
             nc.vector.tensor_copy(g2[:], gt_sb[h][:].indirect(idx2[:]))
             return g2
 
-        def pick_minuend_shared(h):
-            half = J // 2
-            lhalf = half // LIST_ROWS
-            g2 = sb(f"g2_{h}", [P, J], F32)
-            nc.vector.tensor_copy(g2[:, 0:half], gt_sb[h][:].indirect(idx2[:, 0:lhalf]))
-            nc.scalar.activation(g2[:, half:J], gt_sb[h][:].indirect(idx2[:, lhalf : 2 * lhalf]), COPY)
-            return g2
-
-        def turn_adding(g2, g3):
-            bank = psum.tile([P, PACK, P], F32, name="g_turned0", tag="g_turned")
+        def turn_adding(h, g2, g3):
+            bank = psum.tile([P, PACK, P], F32, name=f"g_turned{h}", tag=f"g_turned{h}")
             for t in range(PACK):
                 nc.tensor.matmul(bank[:, t, :], g2[:, t::PACK], ident[:], start=True, stop=False, is_transpose=True)
                 nc.tensor.matmul(bank[:, t, :], g3[:, t::PACK], ident[:], start=False, stop=True, is_transpose=True)
-            return bank
-
-        def add_then_turn(g2, g3):
-            total = sb("g_total", [P, PACK, P], F32)
-            nc.vector.tensor_tensor(
-                total[:].rearrange("p t q -> p q t"),
-                g2[:].rearrange("p (q t) -> p q t", t=PACK),
-                g3[:].rearrange("p (q t) -> p q t", t=PACK),
-                ADD,
-            )
-            bank = psum.tile([P, PACK, P], F32, name="g_turned1", tag="g_turned")
-            for t in range(PACK):
-                nc.tensor.transpose(bank[:, t, :], total[:, t, :], ident[:])
             return bank
 
         def weigh_gradients(h, bank):
@@ -179,29 +154,38 @@ def tile_list_directions_offset_differences_placed_kernel(
                 out=g_codes[h][:].bitcast(E5M2), scales=g_plane[h][:], in_=gj[:].rearrange("p n t -> p (n t)")
             )
 
-        def subtract_features(t):
+        def pieces(total, count):
+            width = total // count
+            return [slice(i * width, (i + 1) * width) for i in range(count)]
+
+        def weigh_features(t):
             picked = sb(f"picked{t}", [P, J], F32)
             diff = sb(f"diff{t}", [P, J], F32)
-            if t == 0:
-                half = J // 2
-                lhalf = half // LIST_ROWS
-                nc.vector.tensor_copy(picked[:, 0:half], xf_sb[t][:].indirect(idx[:, 0:lhalf]))
-                nc.scalar.activation(picked[:, half:J], xf_sb[t][:].indirect(idx[:, lhalf : 2 * lhalf]), COPY)
-            else:
-                nc.scalar.activation(picked[:], xf_sb[t][:].indirect(idx[:]), COPY)
-            nc.vector.tensor_tensor(diff[:], picked[:], ow_sb[t][:], SUB)
-            return diff
-
-        def weigh_features(t, diff):
             us = sb(f"us{t}", [P, J], BF16)
-            nc.vector.scalar_tensor_tensor(
-                us[:].rearrange("p (q i) -> p q i", i=PACK),
-                diff[:].rearrange("p (q i) -> p q i", i=PACK),
-                fk_sb[:, t : t + 1],
-                ra_all[:].rearrange("p i q -> p q i"),
-                MULT,
-                MULT,
-            )
+            count = 4 if t == PACK - 1 else 2
+            cuts = list(zip(pieces(J, count), pieces(J // LIST_ROWS, count), pieces(P, count)))
+
+            def weigh(cols, qcols):
+                nc.vector.scalar_tensor_tensor(
+                    us[:, cols].rearrange("p (q i) -> p q i", i=PACK),
+                    diff[:, cols].rearrange("p (q i) -> p q i", i=PACK),
+                    fk_sb[:, t : t + 1],
+                    ra_all[:, :, qcols].rearrange("p i q -> p q i"),
+                    MULT,
+                    MULT,
+                )
+
+            for i, (cols, lcols, qcols) in enumerate(cuts):
+                window = xf_sb[t][:].indirect(idx[:, lcols])
+                if t == 0 and i == 0:
+                    nc.vector.tensor_copy(picked[:, cols], window)
+                else:
+                    nc.scalar.activation(picked[:, cols], window, COPY)
+            for i, (cols, lcols, qcols) in enumerate(cuts):
+                nc.vector.tensor_tensor(diff[:, cols], picked[:, cols], ow_sb[t][:, cols], SUB)
+                if i > 0:
+                    weigh(cuts[i - 1][0], cuts[i - 1][2])
+            weigh(cuts[-1][0], cuts[-1][2])
             bank = psum.tile([P, 2, P], F32, name=f"u_turned{t}", tag=f"u_turned{t % 3}")
             words = us[:].bitcast(F32)
             for u in range(2):
@@ -224,67 +208,57 @@ def tile_list_directions_offset_differences_placed_kernel(
                 stop=True,
             )
 
-        def quantise_moment(h, copy):
-            w_bf = sb(f"w_bf{h}", [P, P, PACK], BF16)
-            copy(w_bf[:], w_acc[h][:].rearrange("p t n -> p n t"))
-            codes = sb(f"w_codes{h}", [P, P], U32)
-            plane = sb(f"w_plane{h}", [P, P], U8)
-            nc.vector.quantize_mx(out=codes[:].bitcast(E5M2), scales=plane[:], in_=w_bf[:].rearrange("p n t -> p (n t)"))
-            return codes, plane
-
-        def second_product(acc, r, codes, plane):
-            rows = slice(r * P, (r + 1) * P)
-            nc.tensor.matmul_mx(
-                out=acc,
-                lhsT=dr_codes[:, rows].bitcast(E5M2),
-                lhsT_scale=dr_plane[:, rows],
-                rhs=codes[:].bitcast(E5M2),
-                rhs_scale=plane[:],
-                start=True,
-                stop=True,
-            )
-
-        list_cols = P // LIST_ROWS
-
-        g_bank = turn_adding(pick_minuend(0), pick_subtrahend(0))
-        u_banks = [weigh_features(0, subtract_features(0))]
-        gj = weigh_gradients(0, g_bank)
-        diff = subtract_features(1)
-        quantise_gradients(0, gj)
-        u_banks.append(weigh_features(1, diff))
-        for t in range(2):
-            diff = subtract_features(t + 2)
-            quantise_features(t, u_banks[t])
-            u_banks.append(weigh_features(t + 2, diff))
-            first_product(t, 0)
-        subtrahend = pick_subtrahend(1)
-        last_bank = add_then_turn(pick_minuend_shared(1), subtrahend)
-        for t in range(2, PACK):
+        g_banks = [turn_adding(h, pick_minuend(h), pick_subtrahend(h)) for h in range(n_tiles)]
+        u_banks = [weigh_features(0)]
+        quantise_gradients(0, weigh_gradients(0, g_banks[0]))
+        u_banks.append(weigh_features(1))
+        u_banks.append(weigh_features(2))
+        quantise_features(0, u_banks[0])
+        first_product(0, 0)
+        u_banks.append(weigh_features(3))
+        gj = weigh_gradients(1, g_banks[1])
+        for t in (1, 2):
             quantise_features(t, u_banks[t])
             first_product(t, 0)
-
-        codes, plane = quantise_moment(0, nc.scalar.copy)
-        acc = psum.tile([P, r_tiles, P], F32, name="v2_first", tag="u_turned1")
-        for r in range(r_tiles):
-            second_product(acc[:, r, :], r, codes, plane)
-        v2_first = sb("v2_first_sb", [P, r_tiles, P], F32)
-        nc.scalar.copy(v2_first[:], acc[:])
-
-        quantise_gradients(1, weigh_gradients(1, last_bank))
-        for t in range(PACK):
+        quantise_gradients(1, gj)
+        for t in range(PACK - 1):
             first_product(t, 1)
-        for r in range(r_tiles):
-            nc.scalar.activation(pages[r][:].indirect(idx4[:, 0:list_cols]), v2_first[:, r, :], COPY)
+        quantise_features(3, u_banks[3])
+        for h in range(n_tiles):
+            first_product(3, h)
 
-        codes, plane = quantise_moment(1, nc.vector.tensor_copy)
-        accs = [psum.tile([P, P], F32, name=f"v2_last{r}", tag=("ra_all", "u_turned2")[r]) for r in range(r_tiles)]
-        v2_last = [sb(f"v2_last_sb{r}", [P, P], F32) for r in range(r_tiles)]
-        for r in range(r_tiles):
-            second_product(accs[r][:], r, codes, plane)
-        nc.vector.tensor_copy(v2_last[0][:], accs[0][:])
-        nc.scalar.copy(v2_last[1][:], accs[1][:])
-        nc.vector.tensor_copy(pages[0][:].indirect(idx4[:, list_cols : 2 * list_cols]), v2_last[0][:])
-        nc.scalar.activation(pages[1][:].indirect(idx4[:, list_cols : 2 * list_cols]), v2_last[1][:], COPY)
+        w_codes = [sb(f"w_codes{h}", [P, P], U32) for h in range(n_tiles)]
+        w_plane = [sb(f"w_plane{h}", [P, P], U8) for h in range(n_tiles)]
+        w_bf = [sb(f"w_bf{h}", [P, P, PACK], BF16) for h in range(n_tiles)]
+        nc.vector.tensor_copy(w_bf[0][:], w_acc[0][:].rearrange("p t n -> p n t"))
+        nc.scalar.copy(w_bf[1][:], w_acc[1][:].rearrange("p t n -> p n t"))
+        for h in range(n_tiles):
+            nc.vector.quantize_mx(
+                out=w_codes[h][:].bitcast(E5M2), scales=w_plane[h][:], in_=w_bf[h][:].rearrange("p n t -> p (n t)")
+            )
+        free_banks = (("g_turned0", "u_turned1"), ("g_turned1", "u_turned2"))
+        v2 = {}
+        for h in range(n_tiles):
+            accs = []
+            for r in range(r_tiles):
+                rows = slice(r * P, (r + 1) * P)
+                acc = psum.tile([P, P], F32, name=f"v2_acc{r}_{h}", tag=free_banks[r][h])
+                nc.tensor.matmul_mx(
+                    out=acc[:],
+                    lhsT=dr_codes[:, rows].bitcast(E5M2),
+                    lhsT_scale=dr_plane[:, rows],
+                    rhs=w_codes[h][:].bitcast(E5M2),
+                    rhs_scale=w_plane[h][:],
+                    start=True,
+                    stop=True,
+                )
+                accs.append(acc)
+                v2[r, h] = sb(f"v2_{r}_{h}", [P, P], F32)
+            nc.vector.tensor_copy(v2[0, h][:], accs[0][:])
+            nc.scalar.copy(v2[1, h][:], accs[1][:])
+        for h, lcols in enumerate(pieces(N // LIST_ROWS, n_tiles)):
+            nc.vector.tensor_copy(pages[0][:].indirect(idx4[:, lcols]), v2[0, h][:])
+            nc.scalar.activation(pages[1][:].indirect(idx4[:, lcols]), v2[1, h][:], COPY)
 
         for r in range(r_tiles):
             for c0, c1 in STORE_CUTS[r]:

from contextlib import ExitStack

import concourse.mybir as mybir

K, J, N, R, T, V, Q = 512, 512, 256, 256, 1024, 1024, 1024
FLOPS = 2 * J * K * N + 2 * K * R * N

F32 = mybir.dt.float32
BF16 = mybir.dt.bfloat16
I32 = mybir.dt.int32
U32 = mybir.dt.uint32
U16 = mybir.dt.uint16
U8 = mybir.dt.uint8
E4M3 = mybir.dt.float8_e4m3fn_x4
E5M2 = mybir.dt.float8_e5m2_x4
MULT = mybir.AluOpType.mult
ADD = mybir.AluOpType.add
SUB = mybir.AluOpType.subtract
COPY = mybir.ActivationFunctionType.Copy

P = 128
PACK = 4
LIST_ROWS = 16
STORE_CUTS = (((0, 512), (512, 1024)), ((0, 512), (512, 896), (896, 1024)))
QUAD = 32
SLOT = 4096
HALF = SLOT // 2
KB = 1024
PLACES = {
    "block": 0, "g3_0": 0,
    "diff0": 2 * KB, "gj0": 2 * KB,
    "diff2": 4 * KB, "u_codes0": 4 * KB,
    "diff3": 6 * KB, "gj1": 6 * KB, "u_codes1": 7 * KB, "u_codes2": 7 * KB + 512,
    "xf2": 12 * KB, "uj0": 12 * KB,
    "xf3": 16 * KB, "uj1": 16 * KB, "uj2": 17 * KB,
    "col": 28 * KB, "page0": 28 * KB,
    "row": 32 * KB, "page1": 32 * KB,
}


def tile_list_directions_offset_differences_placed_kernel(
    tc, xf, ra, ow, gt, rb, fkr, dr_words, dr_scales, old, offs, offs2, offs3, offs4, out
):
    nc = tc.nc
    n_tiles = N // P
    r_tiles = R // P

    with ExitStack() as ctx:
        keep = ctx.enter_context(tc.tile_pool(name="keep", bufs=1))
        psum = ctx.enter_context(tc.psum_pool(name="psum", bufs=1))

        reuse = ctx.enter_context(tc.tile_pool(name="reuse", bufs=1))

        def sb(name, shape, dtype):
            if name in PLACES:
                return reuse.tile(shape, dtype, name=name, align_bytes=64, offset=PLACES[name])
            return keep.tile(shape, dtype, name=name, align_bytes=64)

        idx = sb("idx", [P, J // LIST_ROWS], U16)
        idx2 = sb("idx2", [P, J // LIST_ROWS], U16)
        idx3 = sb("idx3", [P, J // LIST_ROWS], U16)
        idx4 = sb("idx4", [P, N // LIST_ROWS], U16)
        gt_sb = [sb(f"gt{h}", [P, V], F32) for h in range(n_tiles)]
        xf_sb = [sb(f"xf{t}", [P, T], F32) for t in range(PACK)]
        ow_sb = [sb(f"ow{t}", [P, J], F32) for t in range(PACK)]
        old_sb = [sb(f"old{r}", [P, Q], F32) for r in range(r_tiles)]
        ra_sb = sb("ra_sb", [P, PACK], F32)
        rb_sb = sb("rb_sb", [P, PACK], F32)
        fk_sb = sb("fk_sb", [P, PACK], F32)
        dr_codes = sb("dr_codes", [P, R], U32)
        dr_plane = sb("dr_plane", [P, R], U8)
        ident = sb("ident", [P, P], F32)
        pages = [sb(f"page{r}", [P, Q], F32) for r in range(r_tiles)]

        ones = sb("ones", [P, QUAD], F32)
        col = sb("col", [P, QUAD], F32)
        row = sb("row", [P, QUAD], F32)
        block = sb("block", [P, QUAD], F32)
        nc.vector.memset(ones[:], 1.0)
        nc.vector.memset(ident[:], 0.0)
        nc.vector.tensor_tensor_scan(col[:], ones[:], ones[:], 0.0, MULT, ADD)
        nc.vector.transpose(row[:], col[:])
        nc.vector.tensor_tensor(block[:], col[:], row[:], mybir.AluOpType.is_equal)
        for quad in range(P // QUAD):
            part = slice(quad * QUAD, (quad + 1) * QUAD)
            nc.scalar.activation(ident[part, part], block[part, :], COPY)
        nc.gpsimd.memset(dr_plane[:].bitcast(I32), 0)
        for r in range(r_tiles):
            nc.vector.memset(pages[r][:], 0.0)

        xf_rows = xf.rearrange("(p t) c -> t p c", t=PACK)
        ow_rows = ow.rearrange("(p t) c -> t p c", t=PACK)
        nc.sync.dma_start(out=ra_sb[:], in_=ra.rearrange("o (p t) -> (o p) t", t=PACK))
        nc.sync.dma_start(out=idx3[:], in_=offs3)
        nc.sync.dma_start(out=idx2[:], in_=offs2)
        for h in range(n_tiles):
            nc.sync.dma_start(out=gt_sb[h][:], in_=gt[h * P : (h + 1) * P, :])
        nc.sync.dma_start(out=idx[:], in_=offs)
        nc.sync.dma_start(out=xf_sb[0][:], in_=xf_rows[0])
        nc.sync.dma_start(out=ow_sb[0][:], in_=ow_rows[0])
        nc.sync.dma_start(out=rb_sb[:], in_=rb.rearrange("o (p t) -> (o p) t", t=PACK))
        nc.sync.dma_start(out=fk_sb[:], in_=fkr.rearrange("o (p t) -> (o p) t", t=PACK))
        for t in range(1, PACK):
            nc.sync.dma_start(out=xf_sb[t][:], in_=xf_rows[t])
            nc.sync.dma_start(out=ow_sb[t][:], in_=ow_rows[t])
        nc.sync.dma_start(out=idx4[:], in_=offs4)
        nc.sync.dma_start(
            out=dr_codes[:].bitcast(I32), in_=dr_words[0].rearrange("p c b -> p (c b)").bitcast(I32)
        )
        for quad in range(4):
            nc.sync.dma_start(
                out=dr_plane[32 * quad : 32 * quad + 4, :].bitcast(I32),
                in_=dr_scales[0, 4 * quad : 4 * quad + 4, :].bitcast(I32),
            )
        for r in range(r_tiles):
            nc.sync.dma_start(out=old_sb[r][:], in_=old[r * P : (r + 1) * P, :])

        ra_all = psum.tile([P, PACK, P], F32, name="ra_all", tag="ra_all")
        for t in range(PACK):
            nc.tensor.transpose(ra_all[:, t, :], ra_sb[:, t : t + 1].to_broadcast([P, P]), ident[:])

        g_codes = [sb(f"g_codes{h}", [P, P], U32) for h in range(n_tiles)]
        g_plane = [sb(f"g_plane{h}", [P, P], U8) for h in range(n_tiles)]
        u_codes = [sb(f"u_codes{t}", [P, P], U32) for t in range(PACK)]
        u_plane = [sb(f"u_plane{t}", [P, P], U8) for t in range(PACK)]
        w_acc = [psum.tile([P, PACK, P], F32, name=f"w_acc{h}") for h in range(n_tiles)]

        def pick_subtrahend(h):
            g3 = sb(f"g3_{h}", [P, J], F32)
            nc.scalar.activation(g3[:], gt_sb[h][:].indirect(idx3[:]), COPY, scale=-0.7)
            return g3

        def pick_minuend(h):
            g2 = sb(f"g2_{h}", [P, J], F32)
            nc.vector.tensor_copy(g2[:], gt_sb[h][:].indirect(idx2[:]))
            return g2

        def turn_adding(h, g2, g3):
            bank = psum.tile([P, PACK, P], F32, name=f"g_turned{h}", tag=f"g_turned{h}")
            for t in range(PACK):
                nc.tensor.matmul(bank[:, t, :], g2[:, t::PACK], ident[:], start=True, stop=False, is_transpose=True)
                nc.tensor.matmul(bank[:, t, :], g3[:, t::PACK], ident[:], start=False, stop=True, is_transpose=True)
            return bank

        def weigh_gradients(h, bank):
            gj = sb(f"gj{h}", [P, P, PACK], BF16)
            nc.vector.tensor_tensor(
                gj[:], bank[:].rearrange("p t n -> p n t"), rb_sb[:].unsqueeze(1).to_broadcast([P, P, PACK]), MULT
            )
            return gj

        def quantise_gradients(h, gj):
            nc.vector.quantize_mx(
                out=g_codes[h][:].bitcast(E5M2), scales=g_plane[h][:], in_=gj[:].rearrange("p n t -> p (n t)")
            )

        def pieces(total, count):
            width = total // count
            return [slice(i * width, (i + 1) * width) for i in range(count)]

        def weigh_features(t):
            picked = sb(f"picked{t}", [P, J], F32)
            diff = sb(f"diff{t}", [P, J], F32)
            us = sb(f"us{t}", [P, J], BF16)
            count = 4 if t == PACK - 1 else 2
            cuts = list(zip(pieces(J, count), pieces(J // LIST_ROWS, count), pieces(P, count)))

            def weigh(cols, qcols):
                nc.vector.scalar_tensor_tensor(
                    us[:, cols].rearrange("p (q i) -> p q i", i=PACK),
                    diff[:, cols].rearrange("p (q i) -> p q i", i=PACK),
                    fk_sb[:, t : t + 1],
                    ra_all[:, :, qcols].rearrange("p i q -> p q i"),
                    MULT,
                    MULT,
                )

            for i, (cols, lcols, qcols) in enumerate(cuts):
                window = xf_sb[t][:].indirect(idx[:, lcols])
                if t == 0 and i == 0:
                    nc.vector.tensor_copy(picked[:, cols], window)
                else:
                    nc.scalar.activation(picked[:, cols], window, COPY)
            for i, (cols, lcols, qcols) in enumerate(cuts):
                nc.vector.tensor_tensor(diff[:, cols], picked[:, cols], ow_sb[t][:, cols], SUB)
                if i > 0:
                    weigh(cuts[i - 1][0], cuts[i - 1][2])
            weigh(cuts[-1][0], cuts[-1][2])
            bank = psum.tile([P, 2, P], F32, name=f"u_turned{t}", tag=f"u_turned{t % 3}")
            words = us[:].bitcast(F32)
            for u in range(2):
                nc.tensor.transpose(bank[:, u, :], words[:, u::2], ident[:])
            return bank

        def quantise_features(t, bank):
            uj = sb(f"uj{t}", [P, P * PACK], BF16)
            nc.scalar.copy(uj[:].bitcast(F32).rearrange("p (k u) -> p k u", u=2), bank[:].rearrange("p u k -> p k u"))
            nc.vector.quantize_mx(out=u_codes[t][:].bitcast(E4M3), scales=u_plane[t][:], in_=uj[:])

        def first_product(t, h):
            nc.tensor.matmul_mx(
                out=w_acc[h][:, t, :],
                lhsT=u_codes[t][:].bitcast(E4M3),
                lhsT_scale=u_plane[t][:],
                rhs=g_codes[h][:].bitcast(E5M2),
                rhs_scale=g_plane[h][:],
                start=True,
                stop=True,
            )

        g_banks = [turn_adding(h, pick_minuend(h), pick_subtrahend(h)) for h in range(n_tiles)]
        u_banks = [weigh_features(0)]
        quantise_gradients(0, weigh_gradients(0, g_banks[0]))
        u_banks.append(weigh_features(1))
        u_banks.append(weigh_features(2))
        quantise_features(0, u_banks[0])
        first_product(0, 0)
        u_banks.append(weigh_features(3))
        gj = weigh_gradients(1, g_banks[1])
        for t in (1, 2):
            quantise_features(t, u_banks[t])
            first_product(t, 0)
        quantise_gradients(1, gj)
        for t in range(PACK - 1):
            first_product(t, 1)
        quantise_features(3, u_banks[3])
        for h in range(n_tiles):
            first_product(3, h)

        w_codes = [sb(f"w_codes{h}", [P, P], U32) for h in range(n_tiles)]
        w_plane = [sb(f"w_plane{h}", [P, P], U8) for h in range(n_tiles)]
        w_bf = [sb(f"w_bf{h}", [P, P, PACK], BF16) for h in range(n_tiles)]
        nc.vector.tensor_copy(w_bf[0][:], w_acc[0][:].rearrange("p t n -> p n t"))
        nc.scalar.copy(w_bf[1][:], w_acc[1][:].rearrange("p t n -> p n t"))
        for h in range(n_tiles):
            nc.vector.quantize_mx(
                out=w_codes[h][:].bitcast(E5M2), scales=w_plane[h][:], in_=w_bf[h][:].rearrange("p n t -> p (n t)")
            )
        free_banks = (("g_turned0", "u_turned1"), ("g_turned1", "u_turned2"))
        v2 = {}
        for h in range(n_tiles):
            accs = []
            for r in range(r_tiles):
                rows = slice(r * P, (r + 1) * P)
                acc = psum.tile([P, P], F32, name=f"v2_acc{r}_{h}", tag=free_banks[r][h])
                nc.tensor.matmul_mx(
                    out=acc[:],
                    lhsT=dr_codes[:, rows].bitcast(E5M2),
                    lhsT_scale=dr_plane[:, rows],
                    rhs=w_codes[h][:].bitcast(E5M2),
                    rhs_scale=w_plane[h][:],
                    start=True,
                    stop=True,
                )
                accs.append(acc)
                v2[r, h] = sb(f"v2_{r}_{h}", [P, P], F32)
            nc.vector.tensor_copy(v2[0, h][:], accs[0][:])
            nc.scalar.copy(v2[1, h][:], accs[1][:])
        for h, lcols in enumerate(pieces(N // LIST_ROWS, n_tiles)):
            nc.vector.tensor_copy(pages[0][:].indirect(idx4[:, lcols]), v2[0, h][:])
            nc.scalar.activation(pages[1][:].indirect(idx4[:, lcols]), v2[1, h][:], COPY)

        for r in range(r_tiles):
            for c0, c1 in STORE_CUTS[r]:
                cols = slice(c0, c1)
                res = sb(f"res{r}_{c0}", [P, c1 - c0], F32)
                nc.vector.scalar_tensor_tensor(res[:], pages[r][:, cols], 0.05, old_sb[r][:, cols], MULT, ADD)
                nc.sync.dma_start(out=out[r * P : (r + 1) * P, cols], in_=res[:])
